import numpy as np
import ml_dtypes


def mxq(x, axis, fmt="e4m3"):
    dtype, down = {"e4m3": (ml_dtypes.float8_e4m3fn, 7), "e5m2": (ml_dtypes.float8_e5m2, 14)}[fmt]
    v = np.moveaxis(np.asarray(x, np.float32).astype(ml_dtypes.bfloat16).astype(np.float64), axis, -1)
    blocks = v.reshape(v.shape[:-1] + (-1, 32))
    amax = np.abs(blocks).max(-1, keepdims=True)
    byte = np.maximum(np.where(amax > 0, np.frexp(amax)[1] - 1 + 127, 0) - down, 1)
    scale = np.exp2(byte - 127.0)
    codes = (blocks / scale).astype(np.float32).astype(dtype).astype(np.float64)
    return np.moveaxis((codes * scale).reshape(v.shape), -1, axis)


WIDE = False


def mx_kscale(k):
    if not WIDE:
        return np.ones(k)
    levels = np.array([10, -10, 5, -5, 0])
    if k % 512:
        return np.exp2(np.random.permutation(np.resize(levels, k // 32))).repeat(32)
    a = np.empty((k // 512, 16))
    for p in range(k // 512):
        a[p, :8] = np.random.permutation(np.resize(levels, 8))
        for g in range(8):
            far = levels[np.abs(levels - a[p, g]) >= 10]
            a[p, g + 8] = far[np.random.randint(len(far))]
    return np.exp2(a.ravel()).repeat(32)


def f64(x):
    return np.asarray(x).astype(np.float64)


def striped(idx):
    return np.tile(np.asarray(idx).reshape(-1, 16).T, (8, 1)).astype(np.uint16)


def unstriped(offs):
    return offs[:16].T.reshape(-1).astype(np.int64)


E2M1 = np.array([0.0, 0.5, 1.0, 1.5, 2.0, 3.0, 4.0, 6.0, -0.0, -0.5, -1.0, -1.5, -2.0, -3.0, -4.0, -6.0])


def pack_weight(w, fmt):
    k, n = w.shape
    w = f64(np.asarray(w, np.float32).astype(ml_dtypes.bfloat16)).reshape(k // 32, 32, n)
    amax = np.abs(w).max(1)
    if fmt == "e4m3":
        byte = np.frexp(amax)[1] - 1 + 127 - 7
    else:
        mant, ex = np.frexp(amax / 6.0)
        byte = np.where(mant > 0.5, ex, ex - 1) + 127
    byte = np.clip(np.where(amax > 0, byte, 1), 1, 254)
    scaled = (w * np.exp2(127.0 - byte)[:, None, :]).reshape(k, n).astype(np.float32)
    by_word = np.ascontiguousarray(scaled.reshape(k // 512, 128, 4, n).transpose(0, 1, 3, 2))
    if fmt == "e4m3":
        words = by_word.astype(ml_dtypes.float8_e4m3fn).view(np.uint8)
    else:
        c = by_word.astype(ml_dtypes.float4_e2m1fn).view(np.uint8) & 0xF
        words = (c[..., 0::2] | (c[..., 1::2] << 4)).reshape(k // 512, 128, 2 * n)
    return np.ascontiguousarray(words), np.ascontiguousarray(byte.astype(np.uint8).reshape(k // 512, 16, n))


def unpack_weight(words, scales, fmt):
    g, _, n = scales.shape
    words = np.ascontiguousarray(words).reshape(g, 128, n, -1)
    if fmt == "e4m3":
        vals = words.view(ml_dtypes.float8_e4m3fn).astype(np.float64)
    else:
        nib = np.empty((g, 128, n, 4), np.uint8)
        nib[..., 0::2] = words & 0xF
        nib[..., 1::2] = words >> 4
        vals = E2M1[nib]
    vals = vals * np.repeat(np.exp2(scales.astype(np.float64) - 127.0), 8, axis=1)[..., None]
    return vals.transpose(0, 1, 3, 2).reshape(g * 512, n)


def bf(x):
    return np.asarray(x, np.float32).astype(ml_dtypes.bfloat16)


def planes(Y):
    r, m = Y.shape
    b = f64(bf(Y)).reshape(r // 32, 32, m)
    amax = np.abs(b).max(1)
    byte = np.clip(np.where(amax > 0, np.frexp(amax)[1] - 1 + 127 - 7, 1), 1, 254)
    codes = (b * np.exp2(127.0 - byte)[:, None, :]).reshape(r, m).astype(np.float32).astype(ml_dtypes.float8_e4m3fn).view(np.uint8)
    words = codes.reshape(r // 512, 128, 4, m).transpose(0, 1, 3, 2)
    return np.ascontiguousarray(words), np.ascontiguousarray(byte.astype(np.uint8).reshape(r // 512, 16, m))


R, D, T, I, U, V = 512, 512, 2048, 256, 1024, 1024


def setup_inputs():
    n = np.random.standard_normal
    idx = np.random.permutation(T)[:I]
    idx2 = np.random.permutation(U)[:I]
    idx3 = np.random.permutation(V)[:I]
    fr = mx_kscale(R)
    latp = pack_weight(n((R, T)) / fr[:, None], "e4m3")
    return {
        "up": (n((R, D)) * 0.8 / np.sqrt(R) * fr[:, None]).astype(np.float32),
        "lat_words": latp[0],
        "lat_scales": latp[1],
        "keys": (n((D, U))).astype(np.float32),
        "rate": (np.random.uniform(0.3, 1.0, (1, I))).astype(np.float32),
        "old": (n((D, V)) * 0.7).astype(np.float32),
        "fade": (np.random.uniform(0.5, 1.0, (1, V))).astype(np.float32),
        "offs": striped(idx),
        "offs2": striped(idx2),
        "offs3": striped(idx3),
    }


def reference(up, lat_words, lat_scales, keys, rate, old, fade, offs, offs2, offs3):
    idx = unstriped(offs)
    idx2 = unstriped(offs2)
    idx3 = unstriped(offs3)
    latu = unpack_weight(lat_words, lat_scales, "e4m3")
    upq = mxq(f64(up), 0, "e4m3")
    latidxg = latu[:, idx]
    z = upq.T @ latidxg
    rm = (f64(keys)[:, idx2] - z) * f64(rate)
    rf = np.zeros((D, V))
    rf[:, idx3] = rm
    y = f64(old) * f64(fade) + rf
    words, scales = planes(y)
    return y, words, scales

@@ -1,0 +1,179 @@
+from contextlib import ExitStack
+
+import concourse.mybir as mybir
+from concourse.masks import make_identity
+
+F32 = mybir.dt.float32
+BF16 = mybir.dt.bfloat16
+U32 = mybir.dt.uint32
+I32 = mybir.dt.int32
+U16 = mybir.dt.uint16
+U8 = mybir.dt.uint8
+FP8X4 = mybir.dt.float8_e4m3fn_x4
+ALU = mybir.AluOpType
+COPY = mybir.ActivationFunctionType.Copy
+
+R, D, T, I, U, V = 512, 512, 2048, 256, 1024, 1024
+P = 128
+PACK = 4
+BANK = 512
+VB = V // P
+IB = I // P
+FLOPS = 2 * R * D * I
+
+
+def tile_attend_remainderstore_pl_kernel(tc, up, lat_words, lat_scales, keys, rate, old, fade,
+                                          offs, offs2, offs3, out_0, out_1, out_2):
+    nc = tc.nc
+    with ExitStack() as ctx:
+        sb = ctx.enter_context(tc.tile_pool(name="sb", bufs=1))
+        ps_t = ctx.enter_context(tc.psum_pool(name="ps_t", bufs=4))
+        ps_a = ctx.enter_context(tc.psum_pool(name="ps_a", bufs=4))
+
+        keys_r = keys.rearrange("(p j) u -> p j u", j=PACK)
+        old_r = old.rearrange("(p j) v -> p j v", j=PACK)
+        out_r = out_0.rearrange("(p j) v -> p j v", j=PACK)
+
+        lat_list = sb.tile([P, I // 16], U16, name="lat_list")
+        key_list = sb.tile([P, I // 16], U16, name="key_list")
+        put_list = sb.tile([P, I // 16], U16, name="put_list")
+        up_raw = sb.tile([P, PACK, D], F32, name="up_raw")
+        lat_w = sb.tile([P, T], I32, name="lat_w")
+        lat_s = sb.tile([P, T], U8, name="lat_s")
+        rows = sb.tile([P, P], F32, name="rows")
+        ident = sb.tile([P, P], F32, name="ident")
+        keys_sb = [sb.tile([P, U], F32, name="keys%d" % j) for j in range(PACK)]
+        old_sb = [sb.tile([P, 2, V], F32, name="old%d" % h) for h in range(2)]
+        rf = [sb.tile([P, V], F32, name="rf%d" % j) for j in range(PACK)]
+
+        nc.vector.memset(lat_s[:].bitcast(I32), 0)
+        nc.gpsimd.memset(rows[:], 0.0)
+        for q in range(4):
+            nc.scalar.dma_start(out=lat_s[32 * q : 32 * q + 4, :].bitcast(I32),
+                                in_=lat_scales[0, 4 * q : 4 * q + 4, :].bitcast(I32))
+        nc.scalar.dma_start(out=rows[VB : VB + IB, :], in_=rate.rearrange("o (b p) -> (o b) p", p=P))
+        nc.scalar.dma_start(out=rows[0:VB, :], in_=fade.rearrange("o (b p) -> (o b) p", p=P))
+
+        nc.sync.dma_start(lat_list[:], offs)
+        nc.sync.dma_start(out=up_raw[:], in_=up.rearrange("(p t) d -> p t d", t=PACK))
+        nc.sync.dma_start(out=lat_w[:], in_=lat_words[0].rearrange("p c t -> p (c t)").bitcast(I32))
+        nc.sync.dma_start(key_list[:], offs2)
+        nc.sync.dma_start(put_list[:], offs3)
+        nc.sync.dma_start(out=keys_sb[0][:], in_=keys_r[:, 0, :])
+        nc.sync.dma_start(out=keys_sb[1][:], in_=keys_r[:, 1, :])
+        nc.sync.dma_start(out=old_sb[0][:], in_=old_r[:, 0:2, :])
+        nc.sync.dma_start(out=keys_sb[2][:], in_=keys_r[:, 2, :])
+        nc.sync.dma_start(out=keys_sb[3][:], in_=keys_r[:, 3, :])
+        nc.sync.dma_start(out=old_sb[1][:], in_=old_r[:, 2:4, :])
+
+        make_identity(nc, ident[:])
+        for j in range(PACK):
+            nc.vector.memset(rf[j][:], 0.0)
+
+        cols_ps = ps_t.tile([P, BANK], F32, name="cols_ps", tag="t")
+        nc.tensor.transpose(cols_ps[:, 0:P], rows[:], ident[:])
+        cols = sb.tile([P, 16], F32, name="cols")
+        nc.scalar.copy(out=cols[:], in_=cols_ps[:, 0:16])
+        rate_ps = ps_t.tile([P, BANK], F32, name="rate_ps", tag="t")
+        for b in range(IB):
+            nc.tensor.transpose(rate_ps[:, b * P : (b + 1) * P],
+                                cols[:, VB + b : VB + b + 1].to_broadcast([P, P]), ident[:])
+        rate_sb = sb.tile([P, I], F32, name="rate_sb")
+        nc.scalar.copy(out=rate_sb[:], in_=rate_ps[:, 0:I])
+
+        up_b = sb.tile([P, PACK * D], BF16, name="up_b", align_bytes=64)
+        up_w = sb.tile([P, D], U32, name="up_w", align_bytes=64)
+        up_s = sb.tile([P, D], U8, name="up_s", align_bytes=64)
+        nc.vector.tensor_copy(out=up_b[:].rearrange("p (j m t) -> p m t j", j=PACK, t=PACK),
+                              in_=up_raw[:].rearrange("p t (m j) -> p m t j", j=PACK))
+        latg_s = sb.tile([P, I], U8, name="latg_s", align_bytes=64)
+        latg_w = sb.tile([P, I], U32, name="latg_w", align_bytes=64)
+        nc.vector.tensor_copy(out=latg_s[:], in_=lat_s[:].indirect(lat_list[:]))
+        nc.vector.quantize_mx(out=up_w[:].bitcast(FP8X4), scales=up_s[:], in_=up_b[:])
+        nc.vector.tensor_copy(out=latg_w[:], in_=lat_w[:].bitcast(U32).indirect(lat_list[:]))
+
+        z_sb = [sb.tile([P, I], F32, name="z%d" % j) for j in range(PACK)]
+        for j in range(PACK):
+            z_ps = ps_t.tile([P, BANK], F32, name="z_ps", tag="t")
+            c = slice(j * P, (j + 1) * P)
+            nc.tensor.matmul_mx(out=z_ps[:, 0:I], lhsT=up_w[:, c].bitcast(FP8X4), lhsT_scale=up_s[:, c],
+                                rhs=latg_w[:].bitcast(FP8X4), rhs_scale=latg_s[:], start=True, stop=True)
+            nc.scalar.copy(out=z_sb[j][:], in_=z_ps[:, 0:I])
+
+        y = [sb.tile([P, 2, V], F32, name="y%d" % h) for h in range(2)]
+        NCH = 2
+        CW = V // NCH
+        yb = [sb.tile([P, CW, PACK], BF16, name="yb%d" % c, align_bytes=64) for c in range(NCH)]
+        y_w = sb.tile([P, V], U32, name="y_w", align_bytes=64)
+        y_s = sb.tile([P, V], U8, name="y_s", align_bytes=64)
+        faded = {}
+
+        def remainder(j):
+            diff = sb.tile([P, I], F32, name="diff%d" % j)
+            nc.vector.tensor_tensor(diff[:], keys_sb[j][:].indirect(key_list[:]), z_sb[j][:], ALU.subtract)
+            return diff
+
+        def put(j, diff):
+            nc.vector.tensor_tensor(rf[j][:].indirect(put_list[:]), diff[:], rate_sb[:], ALU.mult)
+
+        def fade_pair(h):
+            turned = sb.tile([P, VB, 2, P], F32, name="turned%d" % h)
+            for g in range(VB // 2):
+                t_ps = ps_t.tile([P, 2, 2, P], F32, name="t_ps", tag="t")
+                for bb in range(2):
+                    for jj in range(2):
+                        b = 2 * g + bb
+                        nc.tensor.transpose(t_ps[:, bb, jj, :], old_sb[h][:, jj, b * P : (b + 1) * P], ident[:])
+                for bb in range(2):
+                    b = 2 * g + bb
+                    nc.scalar.activation(out=turned[:, b, :, :], in_=t_ps[:, bb, :, :], func=COPY, scale=cols[:, b : b + 1])
+            for jj in range(2):
+                for half in range(2):
+                    a_ps = ps_a.tile([P, BANK], F32, name="a_ps", tag="a")
+                    for k in range(4):
+                        nc.tensor.transpose(a_ps[:, k * P : (k + 1) * P], turned[:, 4 * half + k, jj, :], ident[:])
+                    faded[(2 * h + jj, half)] = a_ps
+
+        def add(j, half):
+            c = slice(half * BANK, (half + 1) * BANK)
+            nc.vector.tensor_tensor(y[j // 2][:, j % 2, c], faded[(j, half)][:], rf[j][:, c], ALU.add)
+
+        def round_pair(h, ch, eng_copy):
+            eng_copy(out=yb[ch][:, :, 2 * h : 2 * h + 2],
+                     in_=y[h][:, :, ch * CW : (ch + 1) * CW].rearrange("p j v -> p v j"))
+
+        def quantise(ch):
+            c = slice(ch * CW, (ch + 1) * CW)
+            nc.vector.quantize_mx(out=y_w[:, c].bitcast(FP8X4), scales=y_s[:, c],
+                                  in_=yb[ch][:].rearrange("p v j -> p (v j)"))
+            nc.sync.dma_start(out=out_1[0].rearrange("p c t -> p (c t)").bitcast(I32)[:, c], in_=y_w[:, c].bitcast(I32))
+
+        d0 = remainder(0)
+        put(0, d0)
+        d1 = remainder(1)
+        put(1, d1)
+        fade_pair(0)
+        d2 = remainder(2)
+        put(2, d2)
+        for j in (0, 1):
+            for half in range(2):
+                add(j, half)
+        nc.sync.dma_start(out=out_r[:, 0:2, :], in_=y[0][:])
+        fade_pair(1)
+        for ch in range(NCH):
+            round_pair(0, ch, nc.scalar.copy)
+        d3 = remainder(3)
+        add(2, 0)
+        add(2, 1)
+        nc.sync.dma_start(out=out_r[:, 2, :], in_=y[1][:, 0, :])
+        put(3, d3)
+        add(3, 0)
+        add(3, 1)
+        nc.sync.dma_start(out=out_r[:, 3, :], in_=y[1][:, 1, :])
+        round_pair(1, 0, nc.scalar.copy)
+        round_pair(1, 1, nc.vector.tensor_copy)
+        quantise(0)
+        quantise(1)
+        for q in range(4):
+            eng = nc.sync if q % 2 == 0 else nc.scalar
+            eng.dma_start(out=out_2[0, 4 * q : 4 * q + 4, :].bitcast(I32), in_=y_s[32 * q : 32 * q + 4, :].bitcast(I32))

@@ -27,8 +27,9 @@ def tile_attend_remainderstore_pl_kernel(tc, up, lat_words, lat_scales, keys, ra
     nc = tc.nc
     with ExitStack() as ctx:
         sb = ctx.enter_context(tc.tile_pool(name="sb", bufs=1))
-        ps_t = ctx.enter_context(tc.psum_pool(name="ps_t", bufs=4))
-        ps_a = ctx.enter_context(tc.psum_pool(name="ps_a", bufs=4))
+        again = ctx.enter_context(tc.tile_pool(name="again", bufs=1))
+        ps_t = ctx.enter_context(tc.psum_pool(name="ps_t", bufs=3))
+        ps_a = ctx.enter_context(tc.psum_pool(name="ps_a", bufs=5))
 
         keys_r = keys.rearrange("(p j) u -> p j u", j=PACK)
         old_r = old.rearrange("(p j) v -> p j v", j=PACK)
@@ -43,49 +44,54 @@ def tile_attend_remainderstore_pl_kernel(tc, up, lat_words, lat_scales, keys, ra
         rows = sb.tile([P, P], F32, name="rows")
         ident = sb.tile([P, P], F32, name="ident")
         keys_sb = [sb.tile([P, U], F32, name="keys%d" % j) for j in range(PACK)]
-        old_sb = [sb.tile([P, 2, V], F32, name="old%d" % h) for h in range(2)]
-        rf = [sb.tile([P, V], F32, name="rf%d" % j) for j in range(PACK)]
+        old_sb = [sb.tile([P, 2, V], F32, name="old0"), again.tile([P, 2, V], F32, name="old1", offset=0)]
+        rf = [sb.tile([P, V], F32, name="rf%d" % j, tag="rf%d" % j) for j in range(PACK)]
+        s_stage = sb.tile([P, T // 4], I32, name="s_stage")
+        rate_c = sb.tile([P, IB], F32, name="rate_c")
 
-        nc.vector.memset(lat_s[:].bitcast(I32), 0)
         nc.gpsimd.memset(rows[:], 0.0)
-        for q in range(4):
-            nc.scalar.dma_start(out=lat_s[32 * q : 32 * q + 4, :].bitcast(I32),
-                                in_=lat_scales[0, 4 * q : 4 * q + 4, :].bitcast(I32))
-        nc.scalar.dma_start(out=rows[VB : VB + IB, :], in_=rate.rearrange("o (b p) -> (o b) p", p=P))
-        nc.scalar.dma_start(out=rows[0:VB, :], in_=fade.rearrange("o (b p) -> (o b) p", p=P))
-
         nc.sync.dma_start(lat_list[:], offs)
+        for q in range(4):
+            eng = nc.scalar if q < 2 else nc.sync
+            eng.dma_start(out=s_stage[32 * q : 32 * q + 4, :], in_=lat_scales[0, 4 * q : 4 * q + 4, :].bitcast(I32))
         nc.sync.dma_start(out=up_raw[:], in_=up.rearrange("(p t) d -> p t d", t=PACK))
         nc.sync.dma_start(out=lat_w[:], in_=lat_words[0].rearrange("p c t -> p (c t)").bitcast(I32))
         nc.sync.dma_start(key_list[:], offs2)
-        nc.sync.dma_start(put_list[:], offs3)
         nc.sync.dma_start(out=keys_sb[0][:], in_=keys_r[:, 0, :])
-        nc.sync.dma_start(out=keys_sb[1][:], in_=keys_r[:, 1, :])
+        nc.sync.dma_start(out=rate_c[:], in_=rate.rearrange("o (p b) -> (o p) b", b=IB))
+        nc.sync.dma_start(out=rows[0:VB, :], in_=fade.rearrange("o (b p) -> (o b) p", p=P))
+        nc.sync.dma_start(put_list[:], offs3)
         nc.sync.dma_start(out=old_sb[0][:], in_=old_r[:, 0:2, :])
+        nc.sync.dma_start(out=keys_sb[1][:], in_=keys_r[:, 1, :])
         nc.sync.dma_start(out=keys_sb[2][:], in_=keys_r[:, 2, :])
-        nc.sync.dma_start(out=keys_sb[3][:], in_=keys_r[:, 3, :])
         nc.sync.dma_start(out=old_sb[1][:], in_=old_r[:, 2:4, :])
+        nc.sync.dma_start(out=keys_sb[3][:], in_=keys_r[:, 3, :])
 
         make_identity(nc, ident[:])
+        nc.vector.memset(lat_s[:].bitcast(I32), 0)
+        for q in range(4):
+            nc.vector.tensor_copy(out=lat_s[32 * q : 32 * q + 4, :].bitcast(I32), in_=s_stage[32 * q : 32 * q + 4, :])
         for j in range(PACK):
-            nc.vector.memset(rf[j][:], 0.0)
+            (nc.vector if j < 2 else nc.gpsimd).memset(rf[j][:], 0.0)
 
+        rate_ps = ps_t.tile([P, IB, P], F32, name="rate_ps", tag="t")
+        for b in range(IB):
+            nc.tensor.transpose(rate_ps[:, b, :], rate_c[:, b : b + 1].to_broadcast([P, P]), ident[:])
+        rate_sb = sb.tile([P, I], F32, name="rate_sb")
+        nc.scalar.copy(out=rate_sb[:].rearrange("q (p b) -> q p b", b=IB), in_=rate_ps[:].rearrange("q b p -> q p b"))
         cols_ps = ps_t.tile([P, BANK], F32, name="cols_ps", tag="t")
         nc.tensor.transpose(cols_ps[:, 0:P], rows[:], ident[:])
-        cols = sb.tile([P, 16], F32, name="cols")
-        nc.scalar.copy(out=cols[:], in_=cols_ps[:, 0:16])
-        rate_ps = ps_t.tile([P, BANK], F32, name="rate_ps", tag="t")
-        for b in range(IB):
-            nc.tensor.transpose(rate_ps[:, b * P : (b + 1) * P],
-                                cols[:, VB + b : VB + b + 1].to_broadcast([P, P]), ident[:])
-        rate_sb = sb.tile([P, I], F32, name="rate_sb")
-        nc.scalar.copy(out=rate_sb[:], in_=rate_ps[:, 0:I])
+        cols = sb.tile([P, VB], F32, name="cols")
+        nc.scalar.copy(out=cols[:], in_=cols_ps[:, 0:VB])
 
         up_b = sb.tile([P, PACK * D], BF16, name="up_b", align_bytes=64)
         up_w = sb.tile([P, D], U32, name="up_w", align_bytes=64)
         up_s = sb.tile([P, D], U8, name="up_s", align_bytes=64)
-        nc.vector.tensor_copy(out=up_b[:].rearrange("p (j m t) -> p m t j", j=PACK, t=PACK),
-                              in_=up_raw[:].rearrange("p t (m j) -> p m t j", j=PACK))
+        up_dst = up_b[:].rearrange("p (j m t) -> p m t j", j=PACK, t=PACK)
+        up_src = up_raw[:].rearrange("p t (m j) -> p m t j", j=PACK)
+        MV = 88
+        nc.vector.tensor_copy(out=up_dst[:, 0:MV], in_=up_src[:, 0:MV])
+        nc.scalar.copy(out=up_dst[:, MV:P], in_=up_src[:, MV:P])
         latg_s = sb.tile([P, I], U8, name="latg_s", align_bytes=64)
         latg_w = sb.tile([P, I], U32, name="latg_w", align_bytes=64)
         nc.vector.tensor_copy(out=latg_s[:], in_=lat_s[:].indirect(lat_list[:]))
@@ -98,19 +104,26 @@ def tile_attend_remainderstore_pl_kernel(tc, up, lat_words, lat_scales, keys, ra
             c = slice(j * P, (j + 1) * P)
             nc.tensor.matmul_mx(out=z_ps[:, 0:I], lhsT=up_w[:, c].bitcast(FP8X4), lhsT_scale=up_s[:, c],
                                 rhs=latg_w[:].bitcast(FP8X4), rhs_scale=latg_s[:], start=True, stop=True)
-            nc.scalar.copy(out=z_sb[j][:], in_=z_ps[:, 0:I])
+            if j == 0:
+                z_first = z_ps
+            else:
+                nc.scalar.copy(out=z_sb[j][:], in_=z_ps[:, 0:I])
 
         y = [sb.tile([P, 2, V], F32, name="y%d" % h) for h in range(2)]
-        NCH = 2
-        CW = V // NCH
-        yb = [sb.tile([P, CW, PACK], BF16, name="yb%d" % c, align_bytes=64) for c in range(NCH)]
+        edges = (0, 128, 256, 512, 768, V)
+        NCH = len(edges) - 1
+        yb = [again.tile([P, edges[c + 1] - edges[c], PACK], BF16, name="yb%d" % c, align_bytes=64, offset=edges[c] * PACK * 2) for c in range(NCH)]
         y_w = sb.tile([P, V], U32, name="y_w", align_bytes=64)
         y_s = sb.tile([P, V], U8, name="y_s", align_bytes=64)
         faded = {}
 
         def remainder(j):
-            diff = sb.tile([P, I], F32, name="diff%d" % j)
-            nc.vector.tensor_tensor(diff[:], keys_sb[j][:].indirect(key_list[:]), z_sb[j][:], ALU.subtract)
+            diff = sb.tile([P, I], F32, name="diff%d" % j, tag="rf0" if j == 3 else "diff%d" % j)
+            if j == 0:
+                nc.vector.tensor_copy(out=z_sb[0][:], in_=keys_sb[0][:].indirect(key_list[:]))
+                nc.vector.tensor_tensor(diff[:], z_sb[0][:], z_first[:, 0:I], ALU.subtract)
+            else:
+                nc.vector.tensor_tensor(diff[:], keys_sb[j][:].indirect(key_list[:]), z_sb[j][:], ALU.subtract)
             return diff
 
         def put(j, diff):
@@ -127,26 +140,26 @@ def tile_attend_remainderstore_pl_kernel(tc, up, lat_words, lat_scales, keys, ra
                 for bb in range(2):
                     b = 2 * g + bb
                     nc.scalar.activation(out=turned[:, b, :, :], in_=t_ps[:, bb, :, :], func=COPY, scale=cols[:, b : b + 1])
-            for jj in range(2):
-                for half in range(2):
+            for half in range(2):
+                for jj in range(2):
                     a_ps = ps_a.tile([P, BANK], F32, name="a_ps", tag="a")
                     for k in range(4):
                         nc.tensor.transpose(a_ps[:, k * P : (k + 1) * P], turned[:, 4 * half + k, jj, :], ident[:])
                     faded[(2 * h + jj, half)] = a_ps
 
-        def add(j, half):
-            c = slice(half * BANK, (half + 1) * BANK)
-            nc.vector.tensor_tensor(y[j // 2][:, j % 2, c], faded[(j, half)][:], rf[j][:, c], ALU.add)
+        def add(j, c0, c1):
+            half = c0 // BANK
+            nc.vector.tensor_tensor(y[j // 2][:, j % 2, c0:c1], faded[(j, half)][:, c0 - half * BANK : c1 - half * BANK],
+                                    rf[j][:, c0:c1], ALU.add)
 
         def round_pair(h, ch, eng_copy):
             eng_copy(out=yb[ch][:, :, 2 * h : 2 * h + 2],
-                     in_=y[h][:, :, ch * CW : (ch + 1) * CW].rearrange("p j v -> p v j"))
+                     in_=y[h][:, :, edges[ch] : edges[ch + 1]].rearrange("p j v -> p v j"))
 
         def quantise(ch):
-            c = slice(ch * CW, (ch + 1) * CW)
+            c = slice(edges[ch], edges[ch + 1])
             nc.vector.quantize_mx(out=y_w[:, c].bitcast(FP8X4), scales=y_s[:, c],
                                   in_=yb[ch][:].rearrange("p v j -> p (v j)"))
-            nc.sync.dma_start(out=out_1[0].rearrange("p c t -> p (c t)").bitcast(I32)[:, c], in_=y_w[:, c].bitcast(I32))
 
         d0 = remainder(0)
         put(0, d0)
@@ -155,25 +168,31 @@ def tile_attend_remainderstore_pl_kernel(tc, up, lat_words, lat_scales, keys, ra
         fade_pair(0)
         d2 = remainder(2)
         put(2, d2)
-        for j in (0, 1):
-            for half in range(2):
-                add(j, half)
+        add(0, 0, BANK)
+        add(1, 0, BANK)
+        add(0, BANK, V)
+        d3 = remainder(3)
+        add(1, BANK, V)
         nc.sync.dma_start(out=out_r[:, 0:2, :], in_=y[0][:])
         fade_pair(1)
         for ch in range(NCH):
             round_pair(0, ch, nc.scalar.copy)
-        d3 = remainder(3)
-        add(2, 0)
-        add(2, 1)
-        nc.sync.dma_start(out=out_r[:, 2, :], in_=y[1][:, 0, :])
         put(3, d3)
-        add(3, 0)
-        add(3, 1)
-        nc.sync.dma_start(out=out_r[:, 3, :], in_=y[1][:, 1, :])
-        round_pair(1, 0, nc.scalar.copy)
-        round_pair(1, 1, nc.vector.tensor_copy)
-        quantise(0)
-        quantise(1)
+        for ch in range(NCH):
+            add(2, edges[ch], edges[ch + 1])
+            add(3, edges[ch], edges[ch + 1])
+            if edges[ch + 1] % BANK == 0:
+                c = slice(edges[ch + 1] - BANK, edges[ch + 1])
+                nc.sync.dma_start(out=out_r[:, 2:4, c], in_=y[1][:, :, c])
+            round_pair(1, ch, nc.scalar.copy)
+        words_out = out_1[0].rearrange("p c t -> p (c t)").bitcast(I32)
+        stored = 0
+        for ch in range(NCH):
+            quantise(ch)
+            if edges[ch + 1] >= BANK:
+                c = slice(stored, edges[ch + 1])
+                nc.sync.dma_start(out=words_out[:, c], in_=y_w[:, c].bitcast(I32))
+                stored = edges[ch + 1]
         for q in range(4):
             eng = nc.sync if q % 2 == 0 else nc.scalar
             eng.dma_start(out=out_2[0, 4 * q : 4 * q + 4, :].bitcast(I32), in_=y_s[32 * q : 32 * q + 4, :].bitcast(I32))

@@ -14,12 +14,21 @@ ALU = mybir.AluOpType
 COPY = mybir.ActivationFunctionType.Copy
 
 R, D, T, I, U, V = 512, 512, 2048, 256, 1024, 1024
+FLOPS = 2 * R * D * I
+
 P = 128
 PACK = 4
 BANK = 512
-VB = V // P
-IB = I // P
-FLOPS = 2 * R * D * I
+QUADS = 4
+V_BLOCKS = V // P
+RATE_RUN = I // P
+PAIR_BYTES = 2 * V * 4
+
+SHORT_BANKS, FADED_BANKS = 3, 5
+UP_GROUPS_ON_VECTOR = 88
+EDGES = (0, 128, 256, 512, 768, V)
+CHUNKS = len(EDGES) - 1
+VECTOR_ROUNDS_FROM = V - P
 
 
 def tile_attend_remainderstore_pl_kernel(tc, up, lat_words, lat_scales, keys, rate, old, fade,
@@ -27,13 +36,14 @@ def tile_attend_remainderstore_pl_kernel(tc, up, lat_words, lat_scales, keys, ra
     nc = tc.nc
     with ExitStack() as ctx:
         sb = ctx.enter_context(tc.tile_pool(name="sb", bufs=1))
-        again = ctx.enter_context(tc.tile_pool(name="again", bufs=1))
-        ps_t = ctx.enter_context(tc.psum_pool(name="ps_t", bufs=3))
-        ps_a = ctx.enter_context(tc.psum_pool(name="ps_a", bufs=5))
+        shared = ctx.enter_context(tc.tile_pool(name="shared", bufs=1))
+        ps_short = ctx.enter_context(tc.psum_pool(name="ps_short", bufs=SHORT_BANKS))
+        ps_faded = ctx.enter_context(tc.psum_pool(name="ps_faded", bufs=FADED_BANKS))
 
-        keys_r = keys.rearrange("(p j) u -> p j u", j=PACK)
-        old_r = old.rearrange("(p j) v -> p j v", j=PACK)
-        out_r = out_0.rearrange("(p j) v -> p j v", j=PACK)
+        keys_rows = keys.rearrange("(p j) u -> p j u", j=PACK)
+        old_rows = old.rearrange("(p j) v -> p j v", j=PACK)
+        out_rows = out_0.rearrange("(p j) v -> p j v", j=PACK)
+        out_words = out_1[0].rearrange("p c t -> p (c t)").bitcast(I32)
 
         lat_list = sb.tile([P, I // 16], U16, name="lat_list")
         key_list = sb.tile([P, I // 16], U16, name="key_list")
@@ -41,158 +51,160 @@ def tile_attend_remainderstore_pl_kernel(tc, up, lat_words, lat_scales, keys, ra
         up_raw = sb.tile([P, PACK, D], F32, name="up_raw")
         lat_w = sb.tile([P, T], I32, name="lat_w")
         lat_s = sb.tile([P, T], U8, name="lat_s")
-        rows = sb.tile([P, P], F32, name="rows")
+        fade_rows = sb.tile([P, P], F32, name="fade_rows")
         ident = sb.tile([P, P], F32, name="ident")
         keys_sb = [sb.tile([P, U], F32, name="keys%d" % j) for j in range(PACK)]
-        old_sb = [sb.tile([P, 2, V], F32, name="old0"), again.tile([P, 2, V], F32, name="old1", offset=0)]
+        old_sb = [sb.tile([P, 2, V], F32, name="old0"), shared.tile([P, 2, V], F32, name="old1", offset=0)]
         rf = [sb.tile([P, V], F32, name="rf%d" % j, tag="rf%d" % j) for j in range(PACK)]
-        s_stage = sb.tile([P, T // 4], I32, name="s_stage")
-        rate_c = sb.tile([P, IB], F32, name="rate_c")
+        scale_rows = sb.tile([P, T // 4], I32, name="scale_rows")
+        rate_runs = sb.tile([P, RATE_RUN], F32, name="rate_runs")
 
-        nc.gpsimd.memset(rows[:], 0.0)
+        nc.gpsimd.memset(fade_rows[:], 0.0)
         nc.sync.dma_start(lat_list[:], offs)
-        for q in range(4):
-            eng = nc.scalar if q < 2 else nc.sync
-            eng.dma_start(out=s_stage[32 * q : 32 * q + 4, :], in_=lat_scales[0, 4 * q : 4 * q + 4, :].bitcast(I32))
+        for q in range(QUADS):
+            queue = nc.scalar if q < QUADS // 2 else nc.sync
+            queue.dma_start(out=scale_rows[32 * q : 32 * q + 4, :], in_=lat_scales[0, 4 * q : 4 * q + 4, :].bitcast(I32))
         nc.sync.dma_start(out=up_raw[:], in_=up.rearrange("(p t) d -> p t d", t=PACK))
         nc.sync.dma_start(out=lat_w[:], in_=lat_words[0].rearrange("p c t -> p (c t)").bitcast(I32))
         nc.sync.dma_start(key_list[:], offs2)
-        nc.sync.dma_start(out=keys_sb[0][:], in_=keys_r[:, 0, :])
-        nc.sync.dma_start(out=rate_c[:], in_=rate.rearrange("o (p b) -> (o p) b", b=IB))
-        nc.sync.dma_start(out=rows[0:VB, :], in_=fade.rearrange("o (b p) -> (o b) p", p=P))
+        nc.sync.dma_start(out=keys_sb[0][:], in_=keys_rows[:, 0, :])
+        nc.sync.dma_start(out=rate_runs[:], in_=rate.rearrange("o (p b) -> (o p) b", b=RATE_RUN))
+        nc.sync.dma_start(out=fade_rows[0:V_BLOCKS, :], in_=fade.rearrange("o (b p) -> (o b) p", p=P))
         nc.sync.dma_start(put_list[:], offs3)
-        nc.sync.dma_start(out=old_sb[0][:], in_=old_r[:, 0:2, :])
-        nc.sync.dma_start(out=keys_sb[1][:], in_=keys_r[:, 1, :])
-        nc.sync.dma_start(out=keys_sb[2][:], in_=keys_r[:, 2, :])
-        nc.sync.dma_start(out=old_sb[1][:], in_=old_r[:, 2:4, :])
-        nc.sync.dma_start(out=keys_sb[3][:], in_=keys_r[:, 3, :])
+        nc.sync.dma_start(out=old_sb[0][:], in_=old_rows[:, 0:2, :])
+        nc.sync.dma_start(out=keys_sb[1][:], in_=keys_rows[:, 1, :])
+        nc.sync.dma_start(out=old_sb[1][:, :, 0:BANK], in_=old_rows[:, 2:4, 0:BANK])
+        nc.sync.dma_start(out=keys_sb[2][:], in_=keys_rows[:, 2, :])
+        nc.sync.dma_start(out=keys_sb[3][:], in_=keys_rows[:, 3, :])
+        nc.sync.dma_start(out=old_sb[1][:, :, BANK:V], in_=old_rows[:, 2:4, BANK:V])
 
         make_identity(nc, ident[:])
         nc.vector.memset(lat_s[:].bitcast(I32), 0)
-        for q in range(4):
-            nc.vector.tensor_copy(out=lat_s[32 * q : 32 * q + 4, :].bitcast(I32), in_=s_stage[32 * q : 32 * q + 4, :])
+        for q in range(QUADS):
+            nc.vector.tensor_copy(out=lat_s[32 * q : 32 * q + 4, :].bitcast(I32), in_=scale_rows[32 * q : 32 * q + 4, :])
         for j in range(PACK):
-            (nc.vector if j < 2 else nc.gpsimd).memset(rf[j][:], 0.0)
+            (nc.vector if j < PACK // 2 else nc.gpsimd).memset(rf[j][:], 0.0)
 
-        rate_ps = ps_t.tile([P, IB, P], F32, name="rate_ps", tag="t")
-        for b in range(IB):
-            nc.tensor.transpose(rate_ps[:, b, :], rate_c[:, b : b + 1].to_broadcast([P, P]), ident[:])
+        rate_ps = ps_short.tile([P, RATE_RUN, P], F32, name="rate_ps", tag="short")
+        for b in range(RATE_RUN):
+            nc.tensor.transpose(rate_ps[:, b, :], rate_runs[:, b : b + 1].to_broadcast([P, P]), ident[:])
         rate_sb = sb.tile([P, I], F32, name="rate_sb")
-        nc.scalar.copy(out=rate_sb[:].rearrange("q (p b) -> q p b", b=IB), in_=rate_ps[:].rearrange("q b p -> q p b"))
-        cols_ps = ps_t.tile([P, BANK], F32, name="cols_ps", tag="t")
-        nc.tensor.transpose(cols_ps[:, 0:P], rows[:], ident[:])
-        cols = sb.tile([P, VB], F32, name="cols")
-        nc.scalar.copy(out=cols[:], in_=cols_ps[:, 0:VB])
+        nc.scalar.copy(out=rate_sb[:].rearrange("q (p b) -> q p b", b=RATE_RUN), in_=rate_ps[:].rearrange("q b p -> q p b"))
+        fade_ps = ps_short.tile([P, BANK], F32, name="fade_ps", tag="short")
+        nc.tensor.transpose(fade_ps[:, 0:P], fade_rows[:], ident[:])
+        fade_cols = sb.tile([P, V_BLOCKS], F32, name="fade_cols")
+        nc.scalar.copy(out=fade_cols[:], in_=fade_ps[:, 0:V_BLOCKS])
 
         up_b = sb.tile([P, PACK * D], BF16, name="up_b", align_bytes=64)
         up_w = sb.tile([P, D], U32, name="up_w", align_bytes=64)
         up_s = sb.tile([P, D], U8, name="up_s", align_bytes=64)
         up_dst = up_b[:].rearrange("p (j m t) -> p m t j", j=PACK, t=PACK)
         up_src = up_raw[:].rearrange("p t (m j) -> p m t j", j=PACK)
-        MV = 88
-        nc.vector.tensor_copy(out=up_dst[:, 0:MV], in_=up_src[:, 0:MV])
-        nc.scalar.copy(out=up_dst[:, MV:P], in_=up_src[:, MV:P])
-        latg_s = sb.tile([P, I], U8, name="latg_s", align_bytes=64)
-        latg_w = sb.tile([P, I], U32, name="latg_w", align_bytes=64)
-        nc.vector.tensor_copy(out=latg_s[:], in_=lat_s[:].indirect(lat_list[:]))
+        nc.vector.tensor_copy(out=up_dst[:, 0:UP_GROUPS_ON_VECTOR], in_=up_src[:, 0:UP_GROUPS_ON_VECTOR])
+        nc.scalar.copy(out=up_dst[:, UP_GROUPS_ON_VECTOR:P], in_=up_src[:, UP_GROUPS_ON_VECTOR:P])
+        picked_s = sb.tile([P, I], U8, name="picked_s", align_bytes=64)
+        picked_w = sb.tile([P, I], U32, name="picked_w", align_bytes=64)
+        nc.vector.tensor_copy(out=picked_s[:], in_=lat_s[:].indirect(lat_list[:]))
         nc.vector.quantize_mx(out=up_w[:].bitcast(FP8X4), scales=up_s[:], in_=up_b[:])
-        nc.vector.tensor_copy(out=latg_w[:], in_=lat_w[:].bitcast(U32).indirect(lat_list[:]))
+        nc.vector.tensor_copy(out=picked_w[:], in_=lat_w[:].bitcast(U32).indirect(lat_list[:]))
 
-        z_sb = [sb.tile([P, I], F32, name="z%d" % j) for j in range(PACK)]
-        for j in range(PACK):
-            z_ps = ps_t.tile([P, BANK], F32, name="z_ps", tag="t")
+        def product(j):
+            z_ps = ps_short.tile([P, BANK], F32, name="z_ps", tag="short")
             c = slice(j * P, (j + 1) * P)
             nc.tensor.matmul_mx(out=z_ps[:, 0:I], lhsT=up_w[:, c].bitcast(FP8X4), lhsT_scale=up_s[:, c],
-                                rhs=latg_w[:].bitcast(FP8X4), rhs_scale=latg_s[:], start=True, stop=True)
-            if j == 0:
-                z_first = z_ps
-            else:
-                nc.scalar.copy(out=z_sb[j][:], in_=z_ps[:, 0:I])
+                                rhs=picked_w[:].bitcast(FP8X4), rhs_scale=picked_s[:], start=True, stop=True)
+            return z_ps
+
+        keys0_picked = sb.tile([P, I], F32, name="keys0_picked")
+        z_sb = {j: sb.tile([P, I], F32, name="z%d" % j) for j in range(1, PACK)}
+        z0_ps = product(0)
+        for j in range(1, PACK):
+            nc.scalar.copy(out=z_sb[j][:], in_=product(j)[:, 0:I])
 
         y = [sb.tile([P, 2, V], F32, name="y%d" % h) for h in range(2)]
-        edges = (0, 128, 256, 512, 768, V)
-        NCH = len(edges) - 1
-        yb = [again.tile([P, edges[c + 1] - edges[c], PACK], BF16, name="yb%d" % c, align_bytes=64, offset=edges[c] * PACK * 2) for c in range(NCH)]
+        y_b = [shared.tile([P, EDGES[c + 1] - EDGES[c], PACK], BF16, name="y_b%d" % c, align_bytes=64,
+                           offset=EDGES[c] * PACK * 2 + (PAIR_BYTES if EDGES[c] < BANK else 0)) for c in range(CHUNKS)]
         y_w = sb.tile([P, V], U32, name="y_w", align_bytes=64)
         y_s = sb.tile([P, V], U8, name="y_s", align_bytes=64)
         faded = {}
 
-        def remainder(j):
-            diff = sb.tile([P, I], F32, name="diff%d" % j, tag="rf0" if j == 3 else "diff%d" % j)
-            if j == 0:
-                nc.vector.tensor_copy(out=z_sb[0][:], in_=keys_sb[0][:].indirect(key_list[:]))
-                nc.vector.tensor_tensor(diff[:], z_sb[0][:], z_first[:, 0:I], ALU.subtract)
-            else:
-                nc.vector.tensor_tensor(diff[:], keys_sb[j][:].indirect(key_list[:]), z_sb[j][:], ALU.subtract)
+        def first_difference():
+            diff = sb.tile([P, I], F32, name="diff0")
+            nc.vector.tensor_copy(out=keys0_picked[:], in_=keys_sb[0][:].indirect(key_list[:]))
+            nc.vector.tensor_tensor(diff[:], keys0_picked[:], z0_ps[:, 0:I], ALU.subtract)
+            return diff
+
+        def difference(j, tag):
+            diff = sb.tile([P, I], F32, name="diff%d" % j, tag=tag)
+            nc.vector.tensor_tensor(diff[:], keys_sb[j][:].indirect(key_list[:]), z_sb[j][:], ALU.subtract)
             return diff
 
         def put(j, diff):
             nc.vector.tensor_tensor(rf[j][:].indirect(put_list[:]), diff[:], rate_sb[:], ALU.mult)
 
         def fade_pair(h):
-            turned = sb.tile([P, VB, 2, P], F32, name="turned%d" % h)
-            for g in range(VB // 2):
-                t_ps = ps_t.tile([P, 2, 2, P], F32, name="t_ps", tag="t")
-                for bb in range(2):
-                    for jj in range(2):
-                        b = 2 * g + bb
-                        nc.tensor.transpose(t_ps[:, bb, jj, :], old_sb[h][:, jj, b * P : (b + 1) * P], ident[:])
+            turned = sb.tile([P, V_BLOCKS, 2, P], F32, name="turned%d" % h)
+            for g in range(V_BLOCKS // 2):
+                turn_ps = ps_short.tile([P, 2, 2, P], F32, name="turn_ps", tag="short")
                 for bb in range(2):
                     b = 2 * g + bb
-                    nc.scalar.activation(out=turned[:, b, :, :], in_=t_ps[:, bb, :, :], func=COPY, scale=cols[:, b : b + 1])
+                    for jj in range(2):
+                        nc.tensor.transpose(turn_ps[:, bb, jj, :], old_sb[h][:, jj, b * P : (b + 1) * P], ident[:])
+                for bb in range(2):
+                    b = 2 * g + bb
+                    nc.scalar.activation(out=turned[:, b, :, :], in_=turn_ps[:, bb, :, :], func=COPY,
+                                         scale=fade_cols[:, b : b + 1])
+            blocks_a_bank = BANK // P
             for half in range(2):
                 for jj in range(2):
-                    a_ps = ps_a.tile([P, BANK], F32, name="a_ps", tag="a")
-                    for k in range(4):
-                        nc.tensor.transpose(a_ps[:, k * P : (k + 1) * P], turned[:, 4 * half + k, jj, :], ident[:])
-                    faded[(2 * h + jj, half)] = a_ps
+                    faded_ps = ps_faded.tile([P, BANK], F32, name="faded_ps", tag="faded")
+                    for k in range(blocks_a_bank):
+                        nc.tensor.transpose(faded_ps[:, k * P : (k + 1) * P],
+                                            turned[:, blocks_a_bank * half + k, jj, :], ident[:])
+                    faded[(2 * h + jj, half)] = faded_ps
 
         def add(j, c0, c1):
             half = c0 // BANK
             nc.vector.tensor_tensor(y[j // 2][:, j % 2, c0:c1], faded[(j, half)][:, c0 - half * BANK : c1 - half * BANK],
                                     rf[j][:, c0:c1], ALU.add)
 
-        def round_pair(h, ch, eng_copy):
-            eng_copy(out=yb[ch][:, :, 2 * h : 2 * h + 2],
-                     in_=y[h][:, :, edges[ch] : edges[ch + 1]].rearrange("p j v -> p v j"))
+        def round_pair(copy, h, ch, c0, c1):
+            copy(out=y_b[ch][:, c0 - EDGES[ch] : c1 - EDGES[ch], 2 * h : 2 * h + 2],
+                 in_=y[h][:, :, c0:c1].rearrange("p j v -> p v j"))
 
-        def quantise(ch):
-            c = slice(edges[ch], edges[ch + 1])
-            nc.vector.quantize_mx(out=y_w[:, c].bitcast(FP8X4), scales=y_s[:, c],
-                                  in_=yb[ch][:].rearrange("p v j -> p (v j)"))
-
-        d0 = remainder(0)
-        put(0, d0)
-        d1 = remainder(1)
-        put(1, d1)
+        put(0, first_difference())
+        put(1, difference(1, "diff1"))
         fade_pair(0)
-        d2 = remainder(2)
-        put(2, d2)
         add(0, 0, BANK)
         add(1, 0, BANK)
+        diff2 = difference(2, "diff2")
         add(0, BANK, V)
-        d3 = remainder(3)
+        put(2, diff2)
+        diff3 = difference(3, "rf0")
         add(1, BANK, V)
-        nc.sync.dma_start(out=out_r[:, 0:2, :], in_=y[0][:])
+        nc.sync.dma_start(out=out_rows[:, 0:2, :], in_=y[0][:])
         fade_pair(1)
-        for ch in range(NCH):
-            round_pair(0, ch, nc.scalar.copy)
-        put(3, d3)
-        for ch in range(NCH):
-            add(2, edges[ch], edges[ch + 1])
-            add(3, edges[ch], edges[ch + 1])
-            if edges[ch + 1] % BANK == 0:
-                c = slice(edges[ch + 1] - BANK, edges[ch + 1])
-                nc.sync.dma_start(out=out_r[:, 2:4, c], in_=y[1][:, :, c])
-            round_pair(1, ch, nc.scalar.copy)
-        words_out = out_1[0].rearrange("p c t -> p (c t)").bitcast(I32)
+        for ch in range(CHUNKS):
+            round_pair(nc.scalar.copy, 0, ch, EDGES[ch], EDGES[ch + 1])
+        put(3, diff3)
+
+        for ch in range(CHUNKS):
+            c0, c1 = EDGES[ch], EDGES[ch + 1]
+            add(2, c0, c1)
+            add(3, c0, c1)
+            if c1 % BANK == 0:
+                nc.sync.dma_start(out=out_rows[:, 2:4, c1 - BANK : c1], in_=y[1][:, :, c1 - BANK : c1])
+            round_pair(nc.scalar.copy, 1, ch, c0, min(c1, VECTOR_ROUNDS_FROM))
         stored = 0
-        for ch in range(NCH):
-            quantise(ch)
-            if edges[ch + 1] >= BANK:
-                c = slice(stored, edges[ch + 1])
-                nc.sync.dma_start(out=words_out[:, c], in_=y_w[:, c].bitcast(I32))
-                stored = edges[ch + 1]
-        for q in range(4):
-            eng = nc.sync if q % 2 == 0 else nc.scalar
-            eng.dma_start(out=out_2[0, 4 * q : 4 * q + 4, :].bitcast(I32), in_=y_s[32 * q : 32 * q + 4, :].bitcast(I32))
+        for ch in range(CHUNKS):
+            c0, c1 = EDGES[ch], EDGES[ch + 1]
+            nc.vector.quantize_mx(out=y_w[:, c0:c1].bitcast(FP8X4), scales=y_s[:, c0:c1],
+                                  in_=y_b[ch][:].rearrange("p v j -> p (v j)"))
+            if ch == 0:
+                round_pair(nc.vector.tensor_copy, 1, CHUNKS - 1, VECTOR_ROUNDS_FROM, V)
+            if c1 >= BANK:
+                nc.sync.dma_start(out=out_words[:, stored:c1], in_=y_w[:, stored:c1].bitcast(I32))
+                stored = c1
+        for q in range(QUADS):
+            queue = nc.sync if q % 2 == 0 else nc.scalar
+            queue.dma_start(out=out_2[0, 4 * q : 4 * q + 4, :].bitcast(I32), in_=y_s[32 * q : 32 * q + 4, :].bitcast(I32))

from contextlib import ExitStack

import concourse.mybir as mybir
from concourse.masks import make_identity

F32 = mybir.dt.float32
BF16 = mybir.dt.bfloat16
U32 = mybir.dt.uint32
I32 = mybir.dt.int32
U16 = mybir.dt.uint16
U8 = mybir.dt.uint8
FP8X4 = mybir.dt.float8_e4m3fn_x4
ALU = mybir.AluOpType
COPY = mybir.ActivationFunctionType.Copy

R, D, T, I, U, V = 512, 512, 2048, 256, 1024, 1024
FLOPS = 2 * R * D * I

P = 128
PACK = 4
BANK = 512
QUADS = 4
V_BLOCKS = V // P
RATE_RUN = I // P
PAIR_BYTES = 2 * V * 4

SHORT_BANKS, FADED_BANKS = 3, 5
UP_GROUPS_ON_VECTOR = 88
EDGES = (0, 128, 256, 512, 768, V)
CHUNKS = len(EDGES) - 1
VECTOR_ROUNDS_FROM = V - P


def tile_attend_remainderstore_pl_kernel(tc, up, lat_words, lat_scales, keys, rate, old, fade,
                                          offs, offs2, offs3, out_0, out_1, out_2):
    nc = tc.nc
    with ExitStack() as ctx:
        sb = ctx.enter_context(tc.tile_pool(name="sb", bufs=1))
        shared = ctx.enter_context(tc.tile_pool(name="shared", bufs=1))
        ps_short = ctx.enter_context(tc.psum_pool(name="ps_short", bufs=SHORT_BANKS))
        ps_faded = ctx.enter_context(tc.psum_pool(name="ps_faded", bufs=FADED_BANKS))

        keys_rows = keys.rearrange("(p j) u -> p j u", j=PACK)
        old_rows = old.rearrange("(p j) v -> p j v", j=PACK)
        out_rows = out_0.rearrange("(p j) v -> p j v", j=PACK)
        out_words = out_1[0].rearrange("p c t -> p (c t)").bitcast(I32)

        lat_list = sb.tile([P, I // 16], U16, name="lat_list")
        key_list = sb.tile([P, I // 16], U16, name="key_list")
        put_list = sb.tile([P, I // 16], U16, name="put_list")
        up_raw = sb.tile([P, PACK, D], F32, name="up_raw")
        lat_w = sb.tile([P, T], I32, name="lat_w")
        lat_s = sb.tile([P, T], U8, name="lat_s")
        fade_rows = sb.tile([P, P], F32, name="fade_rows")
        ident = sb.tile([P, P], F32, name="ident")
        keys_sb = [sb.tile([P, U], F32, name="keys%d" % j) for j in range(PACK)]
        old_sb = [sb.tile([P, 2, V], F32, name="old0"), shared.tile([P, 2, V], F32, name="old1", offset=0)]
        rf = [sb.tile([P, V], F32, name="rf%d" % j, tag="rf%d" % j) for j in range(PACK)]
        scale_rows = sb.tile([P, T // 4], I32, name="scale_rows")
        rate_runs = sb.tile([P, RATE_RUN], F32, name="rate_runs")

        nc.gpsimd.memset(fade_rows[:], 0.0)
        nc.sync.dma_start(lat_list[:], offs)
        for q in range(QUADS):
            queue = nc.scalar if q < QUADS // 2 else nc.sync
            queue.dma_start(out=scale_rows[32 * q : 32 * q + 4, :], in_=lat_scales[0, 4 * q : 4 * q + 4, :].bitcast(I32))
        nc.sync.dma_start(out=up_raw[:], in_=up.rearrange("(p t) d -> p t d", t=PACK))
        nc.sync.dma_start(out=lat_w[:], in_=lat_words[0].rearrange("p c t -> p (c t)").bitcast(I32))
        nc.sync.dma_start(key_list[:], offs2)
        nc.sync.dma_start(out=keys_sb[0][:], in_=keys_rows[:, 0, :])
        nc.sync.dma_start(out=rate_runs[:], in_=rate.rearrange("o (p b) -> (o p) b", b=RATE_RUN))
        nc.sync.dma_start(out=fade_rows[0:V_BLOCKS, :], in_=fade.rearrange("o (b p) -> (o b) p", p=P))
        nc.sync.dma_start(put_list[:], offs3)
        nc.sync.dma_start(out=old_sb[0][:], in_=old_rows[:, 0:2, :])
        nc.sync.dma_start(out=keys_sb[1][:], in_=keys_rows[:, 1, :])
        nc.sync.dma_start(out=old_sb[1][:, :, 0:BANK], in_=old_rows[:, 2:4, 0:BANK])
        nc.sync.dma_start(out=keys_sb[2][:], in_=keys_rows[:, 2, :])
        nc.sync.dma_start(out=keys_sb[3][:], in_=keys_rows[:, 3, :])
        nc.sync.dma_start(out=old_sb[1][:, :, BANK:V], in_=old_rows[:, 2:4, BANK:V])

        make_identity(nc, ident[:])
        nc.vector.memset(lat_s[:].bitcast(I32), 0)
        for q in range(QUADS):
            nc.vector.tensor_copy(out=lat_s[32 * q : 32 * q + 4, :].bitcast(I32), in_=scale_rows[32 * q : 32 * q + 4, :])
        for j in range(PACK):
            (nc.vector if j < PACK // 2 else nc.gpsimd).memset(rf[j][:], 0.0)

        rate_ps = ps_short.tile([P, RATE_RUN, P], F32, name="rate_ps", tag="short")
        for b in range(RATE_RUN):
            nc.tensor.transpose(rate_ps[:, b, :], rate_runs[:, b : b + 1].to_broadcast([P, P]), ident[:])
        rate_sb = sb.tile([P, I], F32, name="rate_sb")
        nc.scalar.copy(out=rate_sb[:].rearrange("q (p b) -> q p b", b=RATE_RUN), in_=rate_ps[:].rearrange("q b p -> q p b"))
        fade_ps = ps_short.tile([P, BANK], F32, name="fade_ps", tag="short")
        nc.tensor.transpose(fade_ps[:, 0:P], fade_rows[:], ident[:])
        fade_cols = sb.tile([P, V_BLOCKS], F32, name="fade_cols")
        nc.scalar.copy(out=fade_cols[:], in_=fade_ps[:, 0:V_BLOCKS])

        up_b = sb.tile([P, PACK * D], BF16, name="up_b", align_bytes=64)
        up_w = sb.tile([P, D], U32, name="up_w", align_bytes=64)
        up_s = sb.tile([P, D], U8, name="up_s", align_bytes=64)
        up_dst = up_b[:].rearrange("p (j m t) -> p m t j", j=PACK, t=PACK)
        up_src = up_raw[:].rearrange("p t (m j) -> p m t j", j=PACK)
        nc.vector.tensor_copy(out=up_dst[:, 0:UP_GROUPS_ON_VECTOR], in_=up_src[:, 0:UP_GROUPS_ON_VECTOR])
        nc.scalar.copy(out=up_dst[:, UP_GROUPS_ON_VECTOR:P], in_=up_src[:, UP_GROUPS_ON_VECTOR:P])
        picked_s = sb.tile([P, I], U8, name="picked_s", align_bytes=64)
        picked_w = sb.tile([P, I], U32, name="picked_w", align_bytes=64)
        nc.vector.tensor_copy(out=picked_s[:], in_=lat_s[:].indirect(lat_list[:]))
        nc.vector.quantize_mx(out=up_w[:].bitcast(FP8X4), scales=up_s[:], in_=up_b[:])
        nc.vector.tensor_copy(out=picked_w[:], in_=lat_w[:].bitcast(U32).indirect(lat_list[:]))

        def product(j):
            z_ps = ps_short.tile([P, BANK], F32, name="z_ps", tag="short")
            c = slice(j * P, (j + 1) * P)
            nc.tensor.matmul_mx(out=z_ps[:, 0:I], lhsT=up_w[:, c].bitcast(FP8X4), lhsT_scale=up_s[:, c],
                                rhs=picked_w[:].bitcast(FP8X4), rhs_scale=picked_s[:], start=True, stop=True)
            return z_ps

        keys0_picked = sb.tile([P, I], F32, name="keys0_picked")
        z_sb = {j: sb.tile([P, I], F32, name="z%d" % j) for j in range(1, PACK)}
        z0_ps = product(0)
        for j in range(1, PACK):
            nc.scalar.copy(out=z_sb[j][:], in_=product(j)[:, 0:I])

        y = [sb.tile([P, 2, V], F32, name="y%d" % h) for h in range(2)]
        y_b = [shared.tile([P, EDGES[c + 1] - EDGES[c], PACK], BF16, name="y_b%d" % c, align_bytes=64,
                           offset=EDGES[c] * PACK * 2 + (PAIR_BYTES if EDGES[c] < BANK else 0)) for c in range(CHUNKS)]
        y_w = sb.tile([P, V], U32, name="y_w", align_bytes=64)
        y_s = sb.tile([P, V], U8, name="y_s", align_bytes=64)
        faded = {}

        def first_difference():
            diff = sb.tile([P, I], F32, name="diff0")
            nc.vector.tensor_copy(out=keys0_picked[:], in_=keys_sb[0][:].indirect(key_list[:]))
            nc.vector.tensor_tensor(diff[:], keys0_picked[:], z0_ps[:, 0:I], ALU.subtract)
            return diff

        def difference(j, tag):
            diff = sb.tile([P, I], F32, name="diff%d" % j, tag=tag)
            nc.vector.tensor_tensor(diff[:], keys_sb[j][:].indirect(key_list[:]), z_sb[j][:], ALU.subtract)
            return diff

        def put(j, diff):
            nc.vector.tensor_tensor(rf[j][:].indirect(put_list[:]), diff[:], rate_sb[:], ALU.mult)

        def fade_pair(h):
            turned = sb.tile([P, V_BLOCKS, 2, P], F32, name="turned%d" % h)
            for g in range(V_BLOCKS // 2):
                turn_ps = ps_short.tile([P, 2, 2, P], F32, name="turn_ps", tag="short")
                for bb in range(2):
                    b = 2 * g + bb
                    for jj in range(2):
                        nc.tensor.transpose(turn_ps[:, bb, jj, :], old_sb[h][:, jj, b * P : (b + 1) * P], ident[:])
                for bb in range(2):
                    b = 2 * g + bb
                    nc.scalar.activation(out=turned[:, b, :, :], in_=turn_ps[:, bb, :, :], func=COPY,
                                         scale=fade_cols[:, b : b + 1])
            blocks_a_bank = BANK // P
            for half in range(2):
                for jj in range(2):
                    faded_ps = ps_faded.tile([P, BANK], F32, name="faded_ps", tag="faded")
                    for k in range(blocks_a_bank):
                        nc.tensor.transpose(faded_ps[:, k * P : (k + 1) * P],
                                            turned[:, blocks_a_bank * half + k, jj, :], ident[:])
                    faded[(2 * h + jj, half)] = faded_ps

        def add(j, c0, c1):
            half = c0 // BANK
            nc.vector.tensor_tensor(y[j // 2][:, j % 2, c0:c1], faded[(j, half)][:, c0 - half * BANK : c1 - half * BANK],
                                    rf[j][:, c0:c1], ALU.add)

        def round_pair(copy, h, ch, c0, c1):
            copy(out=y_b[ch][:, c0 - EDGES[ch] : c1 - EDGES[ch], 2 * h : 2 * h + 2],
                 in_=y[h][:, :, c0:c1].rearrange("p j v -> p v j"))

        put(0, first_difference())
        put(1, difference(1, "diff1"))
        fade_pair(0)
        add(0, 0, BANK)
        add(1, 0, BANK)
        diff2 = difference(2, "diff2")
        add(0, BANK, V)
        put(2, diff2)
        diff3 = difference(3, "rf0")
        add(1, BANK, V)
        nc.sync.dma_start(out=out_rows[:, 0:2, :], in_=y[0][:])
        fade_pair(1)
        for ch in range(CHUNKS):
            round_pair(nc.scalar.copy, 0, ch, EDGES[ch], EDGES[ch + 1])
        put(3, diff3)

        for ch in range(CHUNKS):
            c0, c1 = EDGES[ch], EDGES[ch + 1]
            add(2, c0, c1)
            add(3, c0, c1)
            if c1 % BANK == 0:
                nc.sync.dma_start(out=out_rows[:, 2:4, c1 - BANK : c1], in_=y[1][:, :, c1 - BANK : c1])
            round_pair(nc.scalar.copy, 1, ch, c0, min(c1, VECTOR_ROUNDS_FROM))
        stored = 0
        for ch in range(CHUNKS):
            c0, c1 = EDGES[ch], EDGES[ch + 1]
            nc.vector.quantize_mx(out=y_w[:, c0:c1].bitcast(FP8X4), scales=y_s[:, c0:c1],
                                  in_=y_b[ch][:].rearrange("p v j -> p (v j)"))
            if ch == 0:
                round_pair(nc.vector.tensor_copy, 1, CHUNKS - 1, VECTOR_ROUNDS_FROM, V)
            if c1 >= BANK:
                nc.sync.dma_start(out=out_words[:, stored:c1], in_=y_w[:, stored:c1].bitcast(I32))
                stored = c1
        for q in range(QUADS):
            queue = nc.sync if q % 2 == 0 else nc.scalar
            queue.dma_start(out=out_2[0, 4 * q : 4 * q + 4, :].bitcast(I32), in_=y_s[32 * q : 32 * q + 4, :].bitcast(I32))
